import numpy as np
import ml_dtypes


def mxq(x, axis, fmt="e4m3"):
    dtype, down = {"e4m3": (ml_dtypes.float8_e4m3fn, 7), "e5m2": (ml_dtypes.float8_e5m2, 14)}[fmt]
    v = np.moveaxis(np.asarray(x, np.float32).astype(ml_dtypes.bfloat16).astype(np.float64), axis, -1)
    blocks = v.reshape(v.shape[:-1] + (-1, 32))
    amax = np.abs(blocks).max(-1, keepdims=True)
    byte = np.maximum(np.where(amax > 0, np.frexp(amax)[1] - 1 + 127, 0) - down, 1)
    scale = np.exp2(byte - 127.0)
    codes = (blocks / scale).astype(np.float32).astype(dtype).astype(np.float64)
    return np.moveaxis((codes * scale).reshape(v.shape), -1, axis)


WIDE = False


def mx_kscale(k):
    if not WIDE:
        return np.ones(k)
    levels = np.array([10, -10, 5, -5, 0])
    if k % 512:
        return np.exp2(np.random.permutation(np.resize(levels, k // 32))).repeat(32)
    a = np.empty((k // 512, 16))
    for p in range(k // 512):
        a[p, :8] = np.random.permutation(np.resize(levels, 8))
        for g in range(8):
            far = levels[np.abs(levels - a[p, g]) >= 10]
            a[p, g + 8] = far[np.random.randint(len(far))]
    return np.exp2(a.ravel()).repeat(32)


BF16 = ml_dtypes.bfloat16


def bf(x):
    return np.asarray(x, np.float32).astype(BF16)


def f64(x):
    return np.asarray(x).astype(np.float64)


E2M1 = np.array([0.0, 0.5, 1.0, 1.5, 2.0, 3.0, 4.0, 6.0, -0.0, -0.5, -1.0, -1.5, -2.0, -3.0, -4.0, -6.0])


def pack_weight(w, fmt):
    k, n = w.shape
    w = f64(bf(w)).reshape(k // 32, 32, n)
    amax = np.abs(w).max(1)
    if fmt == "e4m3":
        byte = np.frexp(amax)[1] - 1 + 127 - 7
    else:
        mant, ex = np.frexp(amax / 6.0)
        byte = np.where(mant > 0.5, ex, ex - 1) + 127
    byte = np.clip(np.where(amax > 0, byte, 1), 1, 254)
    scaled = (w * np.exp2(127.0 - byte)[:, None, :]).reshape(k, n).astype(np.float32)
    by_word = np.ascontiguousarray(scaled.reshape(k // 512, 128, 4, n).transpose(0, 1, 3, 2))
    if fmt == "e4m3":
        words = by_word.astype(ml_dtypes.float8_e4m3fn).view(np.uint8)
    else:
        c = by_word.astype(ml_dtypes.float4_e2m1fn).view(np.uint8) & 0xF
        words = c[..., 0::2] | (c[..., 1::2] << 4)
    return np.ascontiguousarray(words), np.ascontiguousarray(byte.astype(np.uint8).reshape(k // 512, 16, n))


def unpack_weight(words, scales, fmt):
    g, p, n, _ = words.shape
    if fmt == "e4m3":
        vals = np.ascontiguousarray(words).view(ml_dtypes.float8_e4m3fn).astype(np.float64)
    else:
        nib = np.empty((g, p, n, 4), np.uint8)
        nib[..., 0::2] = words & 0xF
        nib[..., 1::2] = words >> 4
        vals = E2M1[nib]
    vals = vals * np.repeat(np.exp2(scales.astype(np.float64) - 127.0), 8, axis=1)[..., None]
    return vals.transpose(0, 1, 3, 2).reshape(g * 512, n)


T, D, F, R = 1024, 1024, 1024, 512


def hadamard_delta(p1, p2):
    return 0.05 * np.tanh(p1) * (1.0 + np.tanh(p2))


def draw0():
    s = mx_kscale(D)
    a, b = mx_kscale(R), mx_kscale(R)
    x = bf(np.random.standard_normal((T, D)) / s[None, :])
    w0 = bf(np.random.standard_normal((D, F)) / np.sqrt(D))
    x1_words, x1_scales = pack_weight((np.random.standard_normal((D, R)) * a[None, :]).T, "e4m3")
    y1_words, y1_scales = pack_weight(np.random.standard_normal((R, F)) / np.sqrt(R) / a[:, None], "e4m3")
    x2_words, x2_scales = pack_weight((np.random.standard_normal((D, R)) * b[None, :]).T, "e4m3")
    y2_words, y2_scales = pack_weight(np.random.standard_normal((R, F)) / np.sqrt(R) / b[:, None], "e4m3")
    return {
        "x": x,
        "w0": w0,
        "x1_words": x1_words,
        "x1_scales": x1_scales,
        "y1_words": y1_words,
        "y1_scales": y1_scales,
        "x2_words": x2_words,
        "x2_scales": x2_scales,
        "y2_words": y2_words,
        "y2_scales": y2_scales,
        "gain": bf((1.0 + 0.1 * np.random.standard_normal(D)) * s),
    }


def core(x, w0, x1_words, x1_scales, y1_words, y1_scales, x2_words, x2_scales, y2_words, y2_scales, gain):
    p1 = unpack_weight(x1_words, x1_scales, "e4m3").T @ unpack_weight(y1_words, y1_scales, "e4m3")
    p2 = unpack_weight(x2_words, x2_scales, "e4m3").T @ unpack_weight(y2_words, y2_scales, "e4m3")
    dw = hadamard_delta(p1, p2)
    w = f64(gain)[:, None] * (f64(w0) + dw)
    return mxq(f64(x), 1, "e4m3") @ mxq(w, 0, "e4m3")


def e4m3fn_bytes(y):
    return np.clip(np.asarray(y, np.float64), -448.0, 448.0).astype(np.float32).astype(ml_dtypes.float8_e4m3fn).view(np.uint8)


def e4m3fn_values(b):
    return np.asarray(b, np.uint8).view(ml_dtypes.float8_e4m3fn).astype(np.float64)


def setup_inputs():
    d = draw0()
    x0 = np.asarray(d['x']).astype(np.float64)
    s = (np.max(np.abs(x0), axis=(0,), keepdims=True) / 448.0).astype(np.float32)
    out = {}
    for k, v in d.items():
        if k == 'x':
            out['x_bytes'] = e4m3fn_bytes(x0 / s.astype(np.float64))
            out['x_scale'] = s
        else:
            out[k] = v
    return out


def reference(x_bytes, x_scale, w0, x1_words, x1_scales, y1_words, y1_scales, x2_words, x2_scales, y2_words, y2_scales, gain):
    return core(e4m3fn_values(x_bytes) * x_scale.astype(np.float64), w0, x1_words, x1_scales, y1_words, y1_scales, x2_words, x2_scales, y2_words, y2_scales, gain)

@@ -1,0 +1,320 @@
+from contextlib import ExitStack
+
+import concourse.mybir as mybir
+from concourse.masks import make_identity
+
+T, D, F, R = 1024, 1024, 1024, 512
+FLOPS = 2 * D * F * R * 2 + 2 * T * D * F
+
+F32 = mybir.dt.float32
+BF16 = mybir.dt.bfloat16
+I32 = mybir.dt.int32
+U32 = mybir.dt.uint32
+U8 = mybir.dt.uint8
+FP8 = mybir.dt.float8_e4m3fn
+FP8X4 = mybir.dt.float8_e4m3fn_x4
+ACT = mybir.ActivationFunctionType
+ALU = mybir.AluOpType
+
+P = 128
+BANK = 512
+WIDTHS = (512, 256, 128, 128)
+CAST = ('v', 's', 's', 's', 's', 's', 's', 's')
+PESUM = ()
+LAG = 2
+NV = 2
+NM = 1
+XLATE = 0
+PERM_G = "vvgg"
+
+
+def tile_fedparatanhhadamardlinear_w8_kernel(
+    tc, x_bytes, x_scale, w0, x1_words, x1_scales, y1_words, y1_scales,
+    x2_words, x2_scales, y2_words, y2_scales, gain, out,
+):
+    nc = tc.nc
+    with ExitStack() as ctx:
+        keep = ctx.enter_context(tc.tile_pool(name="keep", bufs=1))
+        xio = ctx.enter_context(tc.tile_pool(name="xio", bufs=4))
+        acts = ctx.enter_context(tc.tile_pool(name="acts", bufs=8))
+        upd = ctx.enter_context(tc.tile_pool(name="upd", bufs=3))
+        outs = ctx.enter_context(tc.tile_pool(name="outs", bufs=6))
+        ps_p = ctx.enter_context(tc.psum_pool(name="ps_p", bufs=3))
+        ps_gw = ctx.enter_context(tc.psum_pool(name="ps_gw", bufs=2))
+        ps_xo = ctx.enter_context(tc.psum_pool(name="ps_xo", bufs=3))
+
+        scale_tiles = []
+        for i in range(4):
+            tile_s = keep.tile([P, 1024], U8, align_bytes=256, name="sc%d" % i)
+            nc.vector.memset(tile_s[:].bitcast(I32), 0)
+            scale_tiles.append(tile_s)
+        xs1, ys1, xs2, ys2 = scale_tiles
+        warm = keep.tile([P, 1], F32, name="warm")
+        warm_out = keep.tile([P, 1], F32, name="warm_out")
+        nc.vector.memset(warm[:], 0.0)
+        nc.scalar.activation(out=warm_out[:], in_=warm[:], func=ACT.Sigmoid)
+
+        x_rows = x_bytes.rearrange("(r p) k -> p r k", p=P)
+        xb = []
+        for rp in range(4):
+            tile_b = keep.tile([P, 2, 1024], U8, align_bytes=256, name="xb%d" % rp)
+            xb.append(tile_b)
+        xw1 = keep.tile([P, 1024], U32, align_bytes=256, name="xw1")
+        xw2 = keep.tile([P, 1024], U32, align_bytes=256, name="xw2")
+        yw1 = keep.tile([P, 1024], U32, align_bytes=256, name="yw1")
+        yw2 = keep.tile([P, 1024], U32, align_bytes=256, name="yw2")
+
+        def load_x(rp):
+            nc.sync.dma_start(out=xb[rp][:], in_=x_rows[:, 2 * rp : 2 * rp + 2, :])
+
+        def load_scales(tile_s, k, scales):
+            for r in range(4):
+                nc.sync.dma_start(out=tile_s[k + r : P : 32, :].bitcast(I32), in_=scales[0, r:16:4, :].bitcast(I32))
+
+        def load_words(tile_w, words, c0, c1):
+            flat = words[0].rearrange("p n t -> p (n t)")
+            nc.sync.dma_start(out=tile_w[:, c0:c1].bitcast(I32), in_=flat[:, 4 * c0 : 4 * c1].bitcast(I32))
+
+        gn = keep.tile([P, 8], BF16, name="gn")
+        nc.gpsimd.dma_start(out=gn[:].rearrange("p (g t) -> p g t", t=4), in_=gain.rearrange("(g p t) -> p g t", p=P, t=4))
+        xsc = keep.tile([P, 8], F32, name="xsc")
+        nc.gpsimd.dma_start(out=xsc[:].rearrange("p (g t) -> p g t", t=4), in_=x_scale.rearrange("o (g p t) -> p (o g) t", p=P, t=4))
+        load_x(0)
+        load_x(1)
+        load_scales(xs1, 0, x1_scales)
+        load_words(xw1, x1_words, 0, 512)
+        load_words(yw1, y1_words, 0, 512)
+        load_x(2)
+        load_x(3)
+        load_scales(ys1, 0, y1_scales)
+        load_words(xw2, x2_words, 0, 512)
+        load_scales(xs2, 0, x2_scales)
+        load_words(yw2, y2_words, 0, 512)
+        load_scales(ys2, 0, y2_scales)
+        load_words(xw1, x1_words, 512, 1024)
+        load_words(xw2, x2_words, 512, 1024)
+        w0t = keep.tile([P, 8, 1024], BF16, align_bytes=256, name="w0t")
+        w0_rows = w0.rearrange("(g p t) f -> g p t f", p=P, t=4)
+        for h in range(2):
+            for g in range(2):
+                nc.gpsimd.dma_start(out=w0t[:, 4 * g : 4 * g + 4, 512 * h : 512 * h + 512], in_=w0_rows[g][:, :, 512 * h : 512 * h + 512])
+            if h == 0:
+                load_words(yw1, y1_words, 512, 1024)
+                load_words(yw2, y2_words, 512, 1024)
+
+        ident_f = keep.tile([P, P], F32, align_bytes=256, name="ident_f")
+        make_identity(nc, ident_f[:])
+        ident_b = keep.tile([P, P], BF16, align_bytes=256, name="ident_b")
+        make_identity(nc, ident_b[:])
+        diag = keep.tile([P, 8, P], BF16, align_bytes=256, name="diag")
+        nc.gpsimd.tensor_tensor(
+            out=diag[:], in0=ident_b[:].unsqueeze(1).to_broadcast([P, 8, P]),
+            in1=gn[:].unsqueeze(2).to_broadcast([P, 8, P]), op=ALU.mult,
+        )
+        g01 = keep.tile([P, 8], F32, name="g01")
+        nc.vector.tensor_scalar(out=g01[:], in0=gn[:], scalar1=0.1, scalar2=None, op0=ALU.mult)
+
+        xg = keep.tile([P, 2, 4096], BF16, align_bytes=256, name="xg")
+        xq = keep.tile([P, 2, 1024], U32, align_bytes=256, name="xq")
+        xqs = keep.tile([P, 2, 1024], U8, align_bytes=256, name="xqs")
+        xf = {}
+
+        def cast(rt):
+            tile_f = xio.tile([P, 1024], BF16, align_bytes=256, name="xf")
+            src = xb[rt // 2][:, rt % 2, :].bitcast(FP8)
+            if CAST[rt] == "s":
+                nc.scalar.copy(out=tile_f[:], in_=src)
+            elif CAST[rt] == "v":
+                nc.vector.tensor_copy(out=tile_f[:], in_=src)
+            else:
+                nc.gpsimd.tensor_copy(out=tile_f[:], in_=src)
+            xf[rt] = tile_f
+
+        def x_turn(rp, g):
+            bank = ps_xo.tile([P, BANK], F32, name="xo")
+            for r2 in range(2):
+                words = xf[2 * rp + r2][:].bitcast(F32)
+                for u in range(2):
+                    nc.tensor.transpose(
+                        bank[:, 256 * u + 128 * r2 : 256 * u + 128 * r2 + 128],
+                        words[:, 256 * g + u : 256 * (g + 1) : 2], ident_f[:],
+                    )
+            nc.vector.tensor_tensor(
+                out=xg[:, g, 1024 * rp : 1024 * rp + 1024].rearrange("p (r u e) -> p r u e", u=2, e=2),
+                in0=bank[:].bitcast(BF16).rearrange("p (u r e) -> p r u e", u=2, e=2),
+                in1=xsc[:, 4 * g : 4 * g + 4].rearrange("p (u e) -> p u e", e=2).unsqueeze(1).to_broadcast([P, 256, 2, 2]),
+                op=ALU.mult,
+            )
+
+        def x_quant(half, g):
+            cols = slice(512 * half, 512 * half + 512)
+            nc.vector.quantize_mx(
+                out=xq[:, g, cols].bitcast(FP8X4), scales=xqs[:, g, cols],
+                in_=xg[:, g, 2048 * half : 2048 * half + 2048],
+            )
+
+        x1p = keep.tile([P, 1024], U32, align_bytes=256, name="x1p")
+        x2p = keep.tile([P, 1024], U32, align_bytes=256, name="x2p")
+        xsp1 = keep.tile([P, 1024], U8, align_bytes=256, name="xsp1")
+        xsp2 = keep.tile([P, 1024], U8, align_bytes=256, name="xsp2")
+
+        def perm(eng, dst, src, dtype, g):
+            eng.tensor_copy(
+                out=dst[:, 512 * g : 512 * g + 512].bitcast(dtype).rearrange("p (t m) -> p t m", t=4),
+                in_=src[:, 512 * g : 512 * g + 512].bitcast(dtype).rearrange("p (m t) -> p t m", t=4),
+            )
+
+        wq = keep.tile([P, 2, 1024], U32, align_bytes=256, name="wq")
+        wqs = keep.tile([P, 2, 1024], U8, align_bytes=256, name="wqs")
+        out_rows = out.rearrange("(r p) f -> p r f", p=P)
+
+        def unit(g, ts, f0, w):
+            b1 = ps_p.tile([P, BANK], F32, name="pbank")
+            for j, t in enumerate(ts):
+                st = slice(512 * g + 128 * t, 512 * g + 128 * t + 128)
+                nc.tensor.matmul_mx(
+                    out=b1[:, j * w : j * w + w], lhsT=x1p[:, st].bitcast(FP8X4), lhsT_scale=xsp1[:, st],
+                    rhs=yw1[:, f0 : f0 + w].bitcast(FP8X4), rhs_scale=ys1[:, f0 : f0 + w], start=True, stop=True,
+                )
+            t1 = acts.tile([P, BANK], F32, name="t1")
+            nc.scalar.activation(out=t1[:], in_=b1[:], func=ACT.Tanh)
+            b2 = ps_p.tile([P, BANK], F32, name="pbank")
+            for j, t in enumerate(ts):
+                st = slice(512 * g + 128 * t, 512 * g + 128 * t + 128)
+                nc.tensor.matmul_mx(
+                    out=b2[:, j * w : j * w + w], lhsT=x2p[:, st].bitcast(FP8X4), lhsT_scale=xsp2[:, st],
+                    rhs=yw2[:, f0 : f0 + w].bitcast(FP8X4), rhs_scale=ys2[:, f0 : f0 + w], start=True, stop=True,
+                )
+            s2 = acts.tile([P, BANK], F32, name="s2")
+            nc.scalar.activation(out=s2[:], in_=b2[:], func=ACT.Sigmoid, scale=2.0)
+            return t1, s2
+
+        def product(u, t1, s2, g, ts, w):
+            for j, t in enumerate(ts):
+                nc.vector.scalar_tensor_tensor(
+                    out=u[:, t, :], in0=t1[:, j * w : j * w + w], scalar=g01[:, 4 * g + t : 4 * g + t + 1],
+                    in1=s2[:, j * w : j * w + w], op0=ALU.mult, op1=ALU.mult,
+                )
+
+        def add_base(wb, u, g, f0, fb):
+            bank = ps_gw.tile([P, BANK], F32, name="gw")
+            pesum = (f0, g, fb) in PESUM
+            for t in range(4):
+                nc.tensor.matmul(
+                    out=bank[:, 128 * t : 128 * t + 128], lhsT=diag[:, 4 * g + t, :],
+                    rhs=w0t[:, 4 * g + t, f0 + 128 * fb : f0 + 128 * fb + 128], start=True, stop=not pesum,
+                )
+                if pesum:
+                    nc.tensor.matmul(
+                        out=bank[:, 128 * t : 128 * t + 128], lhsT=ident_f[:],
+                        rhs=u[:, t, 128 * fb : 128 * fb + 128], start=False, stop=True,
+                    )
+            if pesum:
+                nc.scalar.copy(
+                    out=wb[:, 512 * fb : 512 * fb + 512].rearrange("p (f t) -> p f t", t=4),
+                    in_=bank[:].rearrange("p (t f) -> p f t", t=4),
+                )
+                return
+            nc.vector.tensor_tensor(
+                out=wb[:, 512 * fb : 512 * fb + 512].rearrange("p (f t) -> p f t", t=4),
+                in0=bank[:].rearrange("p (t f) -> p f t", t=4),
+                in1=u[:, :, 128 * fb : 128 * fb + 128].rearrange("p t f -> p f t"), op=ALU.add,
+            )
+
+        def w_quant(wb, g, f0, w):
+            nc.vector.quantize_mx(out=wq[:, g, f0 : f0 + w].bitcast(FP8X4), scales=wqs[:, g, f0 : f0 + w], in_=wb[:])
+
+        def main(f0, w, b):
+            n_t = BANK // w
+            bank = ps_xo.tile([P, BANK], F32, name="xo")
+            for j in range(n_t):
+                rows = slice(128 * (b * n_t + j), 128 * (b * n_t + j) + 128)
+                for g in range(2):
+                    nc.tensor.matmul_mx(
+                        out=bank[:, j * w : j * w + w], lhsT=xq[:, g, rows].bitcast(FP8X4), lhsT_scale=xqs[:, g, rows],
+                        rhs=wq[:, g, f0 : f0 + w].bitcast(FP8X4), rhs_scale=wqs[:, g, f0 : f0 + w],
+                        start=(g == 0), stop=(g == 1),
+                    )
+            o = outs.tile([P, BANK], F32, name="o")
+            if f0 + w == F and b % 2 == 1:
+                nc.vector.tensor_copy(out=o[:], in_=bank[:])
+            else:
+                nc.scalar.copy(out=o[:], in_=bank[:])
+            nc.sync.dma_start(
+                out=out_rows[:, b * n_t : b * n_t + n_t, f0 : f0 + w], in_=o[:].rearrange("p (j w) -> p j w", w=w),
+            )
+
+        vq = []
+        mq = []
+
+        def x_first(rp):
+            cast(2 * rp)
+            cast(2 * rp + 1)
+            for g in range(2):
+                x_turn(rp, g)
+
+        def perms(g):
+            engs = {"v": nc.vector, "g": nc.gpsimd}
+            ew = engs[PERM_G[2 * g]]
+            es = engs[PERM_G[2 * g + 1]]
+            perm(es, xsp1, xs1, U8, g)
+            perm(ew, x1p, xw1, I32, g)
+            perm(es, xsp2, xs2, U8, g)
+            perm(ew, x2p, xw2, I32, g)
+
+        def drain(queue, n):
+            for i in range(min(n, len(queue))):
+                queue.pop(0)()
+
+        def finish(u, t1, s2, g, ts, f0, w, wb):
+            product(u, t1, s2, g, ts, w)
+            if ts[-1] == 3:
+                for fb in range(w // 128):
+                    vq.append(lambda fb=fb: add_base(wb, u, g, f0, fb))
+                vq.append(lambda: seal(wb, g, f0, w))
+
+        def seal(wb, g, f0, w):
+            w_quant(wb, g, f0, w)
+            if g == 1:
+                for b in range(8 * w // BANK):
+                    mq.append(lambda b=b: main(f0, w, b))
+
+        units = []
+        f0 = 0
+        for w in WIDTHS:
+            n_t = BANK // w
+            for g in range(2):
+                for k in range(4 // n_t):
+                    units.append((g, list(range(k * n_t, k * n_t + n_t)), f0, w))
+            f0 += w
+
+        x_first(0)
+        perms(0)
+        x_first(1)
+        perms(1)
+        for g in range(2):
+            vq.append(lambda g=g: x_quant(0, g))
+        late = []
+        open_tiles = {}
+        for i in range(len(units) + LAG):
+            if i < len(units):
+                g, ts, f0, w = units[i]
+                if ts[0] == 0:
+                    u = upd.tile([P, 4, w], F32, align_bytes=256, name="u")
+                    wb = upd.tile([P, 4 * w], BF16, align_bytes=256, name="wb")
+                    open_tiles[(f0, g)] = (u, wb)
+                u, wb = open_tiles[(f0, g)]
+                t1, s2 = unit(g, ts, f0, w)
+                late.append((u, t1, s2, g, ts, f0, w, wb))
+            if i >= LAG:
+                finish(*late[i - LAG])
+            if i == XLATE:
+                for rp in range(2, 4):
+                    vq.append(lambda rp=rp: x_first(rp))
+                for g in range(2):
+                    vq.append(lambda g=g: x_quant(1, g))
+            drain(vq, NV)
+            drain(mq, NM)
+        while vq or mq:
+            drain(vq, NV)
+            drain(mq, NM)

@@ -25,7 +25,9 @@ LAG = 2
 NV = 2
 NM = 1
 XLATE = 0
-PERM_G = "vvgg"
+GA = ()
+OUTV = 0
+PERM_G = "vvvv"
 
 
 def tile_fedparatanhhadamardlinear_w8_kernel(
@@ -43,12 +45,16 @@ def tile_fedparatanhhadamardlinear_w8_kernel(
         ps_gw = ctx.enter_context(tc.psum_pool(name="ps_gw", bufs=2))
         ps_xo = ctx.enter_context(tc.psum_pool(name="ps_xo", bufs=3))
 
+        ident_f = keep.tile([P, P], F32, align_bytes=256, name="ident_f")
+        make_identity(nc, ident_f[:])
+        ident_b = keep.tile([P, P], BF16, align_bytes=256, name="ident_b")
+        make_identity(nc, ident_b[:])
         scale_tiles = []
-        for i in range(4):
+        for i in range(3):
             tile_s = keep.tile([P, 1024], U8, align_bytes=256, name="sc%d" % i)
             nc.vector.memset(tile_s[:].bitcast(I32), 0)
             scale_tiles.append(tile_s)
-        xs1, ys1, xs2, ys2 = scale_tiles
+        xs, ys1, ys2 = scale_tiles
         warm = keep.tile([P, 1], F32, name="warm")
         warm_out = keep.tile([P, 1], F32, name="warm_out")
         nc.vector.memset(warm[:], 0.0)
@@ -76,19 +82,19 @@ def tile_fedparatanhhadamardlinear_w8_kernel(
             nc.sync.dma_start(out=tile_w[:, c0:c1].bitcast(I32), in_=flat[:, 4 * c0 : 4 * c1].bitcast(I32))
 
         gn = keep.tile([P, 8], BF16, name="gn")
-        nc.gpsimd.dma_start(out=gn[:].rearrange("p (g t) -> p g t", t=4), in_=gain.rearrange("(g p t) -> p g t", p=P, t=4))
+        nc.scalar.dma_start(out=gn[:].rearrange("p (g t) -> p g t", t=4), in_=gain.rearrange("(g p t) -> p g t", p=P, t=4))
         xsc = keep.tile([P, 8], F32, name="xsc")
-        nc.gpsimd.dma_start(out=xsc[:].rearrange("p (g t) -> p g t", t=4), in_=x_scale.rearrange("o (g p t) -> p (o g) t", p=P, t=4))
+        nc.scalar.dma_start(out=xsc[:].rearrange("p (g t) -> p g t", t=4), in_=x_scale.rearrange("o (g p t) -> p (o g) t", p=P, t=4))
         load_x(0)
         load_x(1)
-        load_scales(xs1, 0, x1_scales)
+        load_scales(xs, 0, x1_scales)
         load_words(xw1, x1_words, 0, 512)
         load_words(yw1, y1_words, 0, 512)
         load_x(2)
         load_x(3)
         load_scales(ys1, 0, y1_scales)
         load_words(xw2, x2_words, 0, 512)
-        load_scales(xs2, 0, x2_scales)
+        load_scales(xs, 4, x2_scales)
         load_words(yw2, y2_words, 0, 512)
         load_scales(ys2, 0, y2_scales)
         load_words(xw1, x1_words, 512, 1024)
@@ -97,20 +103,16 @@ def tile_fedparatanhhadamardlinear_w8_kernel(
         w0_rows = w0.rearrange("(g p t) f -> g p t f", p=P, t=4)
         for h in range(2):
             for g in range(2):
-                nc.gpsimd.dma_start(out=w0t[:, 4 * g : 4 * g + 4, 512 * h : 512 * h + 512], in_=w0_rows[g][:, :, 512 * h : 512 * h + 512])
+                nc.sync.dma_start(out=w0t[:, 4 * g : 4 * g + 4, 512 * h : 512 * h + 512], in_=w0_rows[g][:, :, 512 * h : 512 * h + 512])
             if h == 0:
                 load_words(yw1, y1_words, 512, 1024)
                 load_words(yw2, y2_words, 512, 1024)
 
-        ident_f = keep.tile([P, P], F32, align_bytes=256, name="ident_f")
-        make_identity(nc, ident_f[:])
-        ident_b = keep.tile([P, P], BF16, align_bytes=256, name="ident_b")
-        make_identity(nc, ident_b[:])
         diag = keep.tile([P, 8, P], BF16, align_bytes=256, name="diag")
-        nc.gpsimd.tensor_tensor(
-            out=diag[:], in0=ident_b[:].unsqueeze(1).to_broadcast([P, 8, P]),
-            in1=gn[:].unsqueeze(2).to_broadcast([P, 8, P]), op=ALU.mult,
-        )
+        for i in range(8):
+            nc.gpsimd.tensor_scalar(
+                out=diag[:, i, :], in0=ident_b[:], scalar1=gn[:, i : i + 1], scalar2=0.0, op0=ALU.mult, op1=ALU.add,
+            )
         g01 = keep.tile([P, 8], F32, name="g01")
         nc.vector.tensor_scalar(out=g01[:], in0=gn[:], scalar1=0.1, scalar2=None, op0=ALU.mult)
 
@@ -155,8 +157,7 @@ def tile_fedparatanhhadamardlinear_w8_kernel(
 
         x1p = keep.tile([P, 1024], U32, align_bytes=256, name="x1p")
         x2p = keep.tile([P, 1024], U32, align_bytes=256, name="x2p")
-        xsp1 = keep.tile([P, 1024], U8, align_bytes=256, name="xsp1")
-        xsp2 = keep.tile([P, 1024], U8, align_bytes=256, name="xsp2")
+        xsp = keep.tile([P, 1024], U8, align_bytes=256, name="xsp")
 
         def perm(eng, dst, src, dtype, g):
             eng.tensor_copy(
@@ -173,7 +174,7 @@ def tile_fedparatanhhadamardlinear_w8_kernel(
             for j, t in enumerate(ts):
                 st = slice(512 * g + 128 * t, 512 * g + 128 * t + 128)
                 nc.tensor.matmul_mx(
-                    out=b1[:, j * w : j * w + w], lhsT=x1p[:, st].bitcast(FP8X4), lhsT_scale=xsp1[:, st],
+                    out=b1[:, j * w : j * w + w], lhsT=x1p[:, st].bitcast(FP8X4), lhsT_scale=xsp[:, st],
                     rhs=yw1[:, f0 : f0 + w].bitcast(FP8X4), rhs_scale=ys1[:, f0 : f0 + w], start=True, stop=True,
                 )
             t1 = acts.tile([P, BANK], F32, name="t1")
@@ -182,15 +183,24 @@ def tile_fedparatanhhadamardlinear_w8_kernel(
             for j, t in enumerate(ts):
                 st = slice(512 * g + 128 * t, 512 * g + 128 * t + 128)
                 nc.tensor.matmul_mx(
-                    out=b2[:, j * w : j * w + w], lhsT=x2p[:, st].bitcast(FP8X4), lhsT_scale=xsp2[:, st],
+                    out=b2[:, j * w : j * w + w], lhsT=x2p[:, st].bitcast(FP8X4), lhsT_scale=xsp[4:P, st],
                     rhs=yw2[:, f0 : f0 + w].bitcast(FP8X4), rhs_scale=ys2[:, f0 : f0 + w], start=True, stop=True,
                 )
             s2 = acts.tile([P, BANK], F32, name="s2")
             nc.scalar.activation(out=s2[:], in_=b2[:], func=ACT.Sigmoid, scale=2.0)
             return t1, s2
 
-        def product(u, t1, s2, g, ts, w):
+        def product(u, t1, s2, g, ts, w, on_g):
             for j, t in enumerate(ts):
+                if on_g:
+                    nc.gpsimd.tensor_scalar(
+                        out=t1[:, j * w : j * w + w], in0=t1[:, j * w : j * w + w], scalar1=g01[:, 4 * g + t : 4 * g + t + 1],
+                        scalar2=0.0, op0=ALU.mult, op1=ALU.add,
+                    )
+                    nc.gpsimd.tensor_tensor(
+                        out=u[:, t, :], in0=t1[:, j * w : j * w + w], in1=s2[:, j * w : j * w + w], op=ALU.mult,
+                    )
+                    continue
                 nc.vector.scalar_tensor_tensor(
                     out=u[:, t, :], in0=t1[:, j * w : j * w + w], scalar=g01[:, 4 * g + t : 4 * g + t + 1],
                     in1=s2[:, j * w : j * w + w], op0=ALU.mult, op1=ALU.mult,
@@ -236,7 +246,7 @@ def tile_fedparatanhhadamardlinear_w8_kernel(
                         start=(g == 0), stop=(g == 1),
                     )
             o = outs.tile([P, BANK], F32, name="o")
-            if f0 + w == F and b % 2 == 1:
+            if (f0 + w == F and b % 2 == 1) or b < OUTV:
                 nc.vector.tensor_copy(out=o[:], in_=bank[:])
             else:
                 nc.scalar.copy(out=o[:], in_=bank[:])
@@ -246,6 +256,7 @@ def tile_fedparatanhhadamardlinear_w8_kernel(
 
         vq = []
         mq = []
+        later = []
 
         def x_first(rp):
             cast(2 * rp)
@@ -257,21 +268,27 @@ def tile_fedparatanhhadamardlinear_w8_kernel(
             engs = {"v": nc.vector, "g": nc.gpsimd}
             ew = engs[PERM_G[2 * g]]
             es = engs[PERM_G[2 * g + 1]]
-            perm(es, xsp1, xs1, U8, g)
+            perm(es, xsp, xs, U8, g)
             perm(ew, x1p, xw1, I32, g)
-            perm(es, xsp2, xs2, U8, g)
             perm(ew, x2p, xw2, I32, g)
 
         def drain(queue, n):
             for i in range(min(n, len(queue))):
                 queue.pop(0)()
 
-        def finish(u, t1, s2, g, ts, f0, w, wb):
-            product(u, t1, s2, g, ts, w)
+        def drain_v(n):
+            for i in range(min(n, len(vq))):
+                kind, task = vq.pop(0)
+                task()
+                if vq and vq[0][0] == "q" and kind == "b":
+                    return
+
+        def finish(i, u, t1, s2, g, ts, f0, w, wb):
+            product(u, t1, s2, g, ts, w, i in GA)
             if ts[-1] == 3:
                 for fb in range(w // 128):
-                    vq.append(lambda fb=fb: add_base(wb, u, g, f0, fb))
-                vq.append(lambda: seal(wb, g, f0, w))
+                    later.append(("b", lambda fb=fb: add_base(wb, u, g, f0, fb)))
+                later.append(("q", lambda: seal(wb, g, f0, w)))
 
         def seal(wb, g, f0, w):
             w_quant(wb, g, f0, w)
@@ -293,7 +310,7 @@ def tile_fedparatanhhadamardlinear_w8_kernel(
         x_first(1)
         perms(1)
         for g in range(2):
-            vq.append(lambda g=g: x_quant(0, g))
+            vq.append(("q", lambda g=g: x_quant(0, g)))
         late = []
         open_tiles = {}
         for i in range(len(units) + LAG):
@@ -306,15 +323,20 @@ def tile_fedparatanhhadamardlinear_w8_kernel(
                 u, wb = open_tiles[(f0, g)]
                 t1, s2 = unit(g, ts, f0, w)
                 late.append((u, t1, s2, g, ts, f0, w, wb))
+            fresh = list(later)
+            later.clear()
+            vq.extend(fresh)
             if i >= LAG:
-                finish(*late[i - LAG])
+                finish(i - LAG, *late[i - LAG])
             if i == XLATE:
                 for rp in range(2, 4):
-                    vq.append(lambda rp=rp: x_first(rp))
+                    vq.append(("x", lambda rp=rp: x_first(rp)))
                 for g in range(2):
-                    vq.append(lambda g=g: x_quant(1, g))
-            drain(vq, NV)
+                    vq.append(("q", lambda g=g: x_quant(1, g)))
+            drain_v(NV)
             drain(mq, NM)
-        while vq or mq:
-            drain(vq, NV)
+        while vq or mq or later:
+            vq.extend(later)
+            later.clear()
+            drain_v(NV)
             drain(mq, NM)

@@ -19,12 +19,11 @@ ALU = mybir.AluOpType
 P = 128
 BANK = 512
 WIDTHS = (512, 256, 128, 128)
-CAST = ('v', 's', 's', 's', 's', 's', 's', 's')
-PESUM = ()
-LAG = 2
-NV = 2
-NM = 1
-XLATE = 0
+CAST = ("v", "s", "s", "s", "s", "s", "s", "s")
+LEAD = 4
+XSPLIT = 5
+AHEAD = 2
+NMQ = 1
 GA = ()
 OUTV = 0
 PERM_G = "vvvv"
@@ -206,29 +205,23 @@ def tile_fedparatanhhadamardlinear_w8_kernel(
                     in1=s2[:, j * w : j * w + w], op0=ALU.mult, op1=ALU.mult,
                 )
 
-        def add_base(wb, u, g, f0, fb):
+        banks = {}
+
+        def base_bank(g, f0, fb):
             bank = ps_gw.tile([P, BANK], F32, name="gw")
-            pesum = (f0, g, fb) in PESUM
             for t in range(4):
                 nc.tensor.matmul(
                     out=bank[:, 128 * t : 128 * t + 128], lhsT=diag[:, 4 * g + t, :],
-                    rhs=w0t[:, 4 * g + t, f0 + 128 * fb : f0 + 128 * fb + 128], start=True, stop=not pesum,
+                    rhs=w0t[:, 4 * g + t, f0 + 128 * fb : f0 + 128 * fb + 128], start=True, stop=True,
                 )
-                if pesum:
-                    nc.tensor.matmul(
-                        out=bank[:, 128 * t : 128 * t + 128], lhsT=ident_f[:],
-                        rhs=u[:, t, 128 * fb : 128 * fb + 128], start=False, stop=True,
-                    )
-            if pesum:
-                nc.scalar.copy(
-                    out=wb[:, 512 * fb : 512 * fb + 512].rearrange("p (f t) -> p f t", t=4),
-                    in_=bank[:].rearrange("p (t f) -> p f t", t=4),
-                )
-                return
+            banks[(g, f0, fb)] = bank
+
+        def add_base(wb, u, g, f0, fb):
+            bank = banks[(g, f0, fb)]
             nc.vector.tensor_tensor(
-                out=wb[:, 512 * fb : 512 * fb + 512].rearrange("p (f t) -> p f t", t=4),
-                in0=bank[:].rearrange("p (t f) -> p f t", t=4),
-                in1=u[:, :, 128 * fb : 128 * fb + 128].rearrange("p t f -> p f t"), op=ALU.add,
+                out=wb[:, 512 * fb : 512 * fb + 512].rearrange("p (c i t) -> p c t i", i=4, t=4),
+                in0=bank[:].rearrange("p (t c i) -> p c t i", t=4, i=4),
+                in1=u[:, :, 128 * fb : 128 * fb + 128].rearrange("p t (c i) -> p c t i", i=4), op=ALU.add,
             )
 
         def w_quant(wb, g, f0, w):
@@ -254,89 +247,92 @@ def tile_fedparatanhhadamardlinear_w8_kernel(
                 out=out_rows[:, b * n_t : b * n_t + n_t, f0 : f0 + w], in_=o[:].rearrange("p (j w) -> p j w", w=w),
             )
 
-        vq = []
-        mq = []
-        later = []
-
-        def x_first(rp):
-            cast(2 * rp)
-            cast(2 * rp + 1)
-            for g in range(2):
-                x_turn(rp, g)
-
-        def perms(g):
-            engs = {"v": nc.vector, "g": nc.gpsimd}
-            ew = engs[PERM_G[2 * g]]
-            es = engs[PERM_G[2 * g + 1]]
-            perm(es, xsp, xs, U8, g)
-            perm(ew, x1p, xw1, I32, g)
-            perm(ew, x2p, xw2, I32, g)
-
-        def drain(queue, n):
-            for i in range(min(n, len(queue))):
-                queue.pop(0)()
-
-        def drain_v(n):
-            for i in range(min(n, len(vq))):
-                kind, task = vq.pop(0)
-                task()
-                if vq and vq[0][0] == "q" and kind == "b":
-                    return
-
-        def finish(i, u, t1, s2, g, ts, f0, w, wb):
-            product(u, t1, s2, g, ts, w, i in GA)
-            if ts[-1] == 3:
-                for fb in range(w // 128):
-                    later.append(("b", lambda fb=fb: add_base(wb, u, g, f0, fb)))
-                later.append(("q", lambda: seal(wb, g, f0, w)))
-
-        def seal(wb, g, f0, w):
-            w_quant(wb, g, f0, w)
-            if g == 1:
-                for b in range(8 * w // BANK):
-                    mq.append(lambda b=b: main(f0, w, b))
-
+        ctx.enter_context(tc.manual_schedule(engines={mybir.EngineType.DVE}))
         units = []
         f0 = 0
         for w in WIDTHS:
             n_t = BANK // w
             for g in range(2):
-                for k in range(4 // n_t):
-                    units.append((g, list(range(k * n_t, k * n_t + n_t)), f0, w))
+                units.append([(g, list(range(k * n_t, k * n_t + n_t)), f0, w) for k in range(4 // n_t)])
             f0 += w
 
-        x_first(0)
-        perms(0)
-        x_first(1)
-        perms(1)
-        for g in range(2):
-            vq.append(("q", lambda g=g: x_quant(0, g)))
-        late = []
-        open_tiles = {}
-        for i in range(len(units) + LAG):
-            if i < len(units):
-                g, ts, f0, w = units[i]
-                if ts[0] == 0:
-                    u = upd.tile([P, 4, w], F32, align_bytes=256, name="u")
-                    wb = upd.tile([P, 4 * w], BF16, align_bytes=256, name="wb")
-                    open_tiles[(f0, g)] = (u, wb)
-                u, wb = open_tiles[(f0, g)]
-                t1, s2 = unit(g, ts, f0, w)
-                late.append((u, t1, s2, g, ts, f0, w, wb))
-            fresh = list(later)
-            later.clear()
-            vq.extend(fresh)
-            if i >= LAG:
-                finish(i - LAG, *late[i - LAG])
-            if i == XLATE:
-                for rp in range(2, 4):
-                    vq.append(("x", lambda rp=rp: x_first(rp)))
-                for g in range(2):
-                    vq.append(("q", lambda g=g: x_quant(1, g)))
-            drain_v(NV)
-            drain(mq, NM)
-        while vq or mq or later:
-            vq.extend(later)
-            later.clear()
-            drain_v(NV)
-            drain(mq, NM)
+        made = []
+        flat = [a for phase in units for a in phase]
+        tiles = {}
+
+        def make_units(upto):
+            while len(made) < min(upto, len(flat)):
+                made.append(unit(*flat[len(made)]))
+
+        used = []
+
+        def product_next():
+            g, ts, f0, w = flat[len(used)]
+            make_units(len(used) + 1 + LEAD)
+            if ts[0] == 0:
+                u = upd.tile([P, 4, w], F32, align_bytes=256, name="u")
+                wb = upd.tile([P, 4 * w], BF16, align_bytes=256, name="wb")
+                tiles[(f0, g)] = (u, wb)
+            t1, s2 = made[len(used)]
+            product(tiles[(f0, g)][0], t1, s2, g, ts, w, False)
+            used.append(1)
+
+        mq = []
+
+        def seal(f0, w, g):
+            w_quant(tiles[(f0, g)][1], g, f0, w)
+            if g == 1:
+                for b in range(8 * w // BANK):
+                    mq.append(lambda b=b: main(f0, w, b))
+
+        def weave(a, b):
+            res = []
+            for i in range(max(len(a), len(b))):
+                if i < len(a):
+                    res.append(a[i])
+                if i < len(b):
+                    res.append(b[i])
+            return res
+
+        def task(run, ahead=None):
+            return (run, ahead)
+
+        def x_task(rp, g):
+            if g == 0:
+                cast(2 * rp)
+                cast(2 * rp + 1)
+            x_turn(rp, g)
+
+        def perm_task(dst, src, dtype, g):
+            return task(lambda: perm(nc.vector, dst, src, dtype, g))
+
+        turns = [task(lambda rp=rp, g=g: x_task(rp, g)) for rp in range(4) for g in range(2)]
+        perms = [
+            perm_task(dst, src, dtype, g) for g in range(2)
+            for dst, src, dtype in ((xsp, xs, U8), (x1p, xw1, I32), (x2p, xw2, I32))
+        ]
+        seq = turns[:XSPLIT] + perms[:3] + turns[XSPLIT:6] + perms[3:] + [task(lambda g=g: x_quant(0, g)) for g in range(2)]
+        rest = turns[6:] + [task(lambda g=g: x_quant(1, g)) for g in range(2)]
+        carry = []
+        for phase in units:
+            seq += weave([task(product_next) for a in phase], rest)
+            g, ts, f0, w = phase[0]
+            rest = carry + [
+                task(
+                    lambda fb=fb, f0=f0, g=g: add_base(tiles[(f0, g)][1], tiles[(f0, g)][0], g, f0, fb),
+                    lambda fb=fb, f0=f0, g=g: base_bank(g, f0, fb),
+                )
+                for fb in range(w // 128)
+            ]
+            carry = [task(lambda w=w, f0=f0, g=g: seal(f0, w, g))]
+        seq += rest + carry
+        ahead = [(i, a) for i, (run, a) in enumerate(seq) if a]
+        for i, (run, a) in enumerate(seq):
+            while ahead and ahead[0][0] <= i + AHEAD:
+                ahead.pop(0)[1]()
+            run()
+            for j in range(NMQ):
+                if mq:
+                    mq.pop(0)()
+        while mq:
+            mq.pop(0)()

@@ -19,13 +19,16 @@ ALU = mybir.AluOpType
 P = 128
 BANK = 512
 WIDTHS = (512, 256, 128, 128)
-CAST = ("v", "s", "s", "s", "s", "s", "s", "s")
-LEAD = 4
-XSPLIT = 5
+CAST = ("v", "h", "s", "s", "s", "s", "s", "s")
+LEAD = 5
 AHEAD = 2
+CASTS_AHEAD = 0
 NMQ = 1
-GA = ()
-OUTV = 0
+LAST_T = 2
+ORDER = "02 24 a 48 A0 C0 c b B0 D0 d A1 B1"
+PERM_AT = (4, 6)
+XHEAD = 6
+SUM_PE = ((0, 0), (0, 1))
 PERM_G = "vvvv"
 
 
@@ -36,18 +39,14 @@ def tile_fedparatanhhadamardlinear_w8_kernel(
     nc = tc.nc
     with ExitStack() as ctx:
         keep = ctx.enter_context(tc.tile_pool(name="keep", bufs=1))
-        xio = ctx.enter_context(tc.tile_pool(name="xio", bufs=4))
+        xio = ctx.enter_context(tc.tile_pool(name="xio", bufs=8))
         acts = ctx.enter_context(tc.tile_pool(name="acts", bufs=8))
         upd = ctx.enter_context(tc.tile_pool(name="upd", bufs=3))
-        outs = ctx.enter_context(tc.tile_pool(name="outs", bufs=6))
+        outs = ctx.enter_context(tc.tile_pool(name="outs", bufs=10))
         ps_p = ctx.enter_context(tc.psum_pool(name="ps_p", bufs=3))
         ps_gw = ctx.enter_context(tc.psum_pool(name="ps_gw", bufs=2))
         ps_xo = ctx.enter_context(tc.psum_pool(name="ps_xo", bufs=3))
 
-        ident_f = keep.tile([P, P], F32, align_bytes=256, name="ident_f")
-        make_identity(nc, ident_f[:])
-        ident_b = keep.tile([P, P], BF16, align_bytes=256, name="ident_b")
-        make_identity(nc, ident_b[:])
         scale_tiles = []
         for i in range(3):
             tile_s = keep.tile([P, 1024], U8, align_bytes=256, name="sc%d" % i)
@@ -60,17 +59,14 @@ def tile_fedparatanhhadamardlinear_w8_kernel(
         nc.scalar.activation(out=warm_out[:], in_=warm[:], func=ACT.Sigmoid)
 
         x_rows = x_bytes.rearrange("(r p) k -> p r k", p=P)
-        xb = []
-        for rp in range(4):
-            tile_b = keep.tile([P, 2, 1024], U8, align_bytes=256, name="xb%d" % rp)
-            xb.append(tile_b)
+        xb = keep.tile([P, 8, 1024], U8, align_bytes=256, name="xb")
         xw1 = keep.tile([P, 1024], U32, align_bytes=256, name="xw1")
         xw2 = keep.tile([P, 1024], U32, align_bytes=256, name="xw2")
         yw1 = keep.tile([P, 1024], U32, align_bytes=256, name="yw1")
         yw2 = keep.tile([P, 1024], U32, align_bytes=256, name="yw2")
 
-        def load_x(rp):
-            nc.sync.dma_start(out=xb[rp][:], in_=x_rows[:, 2 * rp : 2 * rp + 2, :])
+        def load_x(r0, r1):
+            nc.sync.dma_start(out=xb[:, r0:r1, :], in_=x_rows[:, r0:r1, :])
 
         def load_scales(tile_s, k, scales):
             for r in range(4):
@@ -81,23 +77,22 @@ def tile_fedparatanhhadamardlinear_w8_kernel(
             nc.sync.dma_start(out=tile_w[:, c0:c1].bitcast(I32), in_=flat[:, 4 * c0 : 4 * c1].bitcast(I32))
 
         gn = keep.tile([P, 8], BF16, name="gn")
-        nc.scalar.dma_start(out=gn[:].rearrange("p (g t) -> p g t", t=4), in_=gain.rearrange("(g p t) -> p g t", p=P, t=4))
         xsc = keep.tile([P, 8], F32, name="xsc")
-        nc.scalar.dma_start(out=xsc[:].rearrange("p (g t) -> p g t", t=4), in_=x_scale.rearrange("o (g p t) -> p (o g) t", p=P, t=4))
-        load_x(0)
-        load_x(1)
-        load_scales(xs, 0, x1_scales)
-        load_words(xw1, x1_words, 0, 512)
-        load_words(yw1, y1_words, 0, 512)
-        load_x(2)
-        load_x(3)
-        load_scales(ys1, 0, y1_scales)
-        load_words(xw2, x2_words, 0, 512)
-        load_scales(xs, 4, x2_scales)
-        load_words(yw2, y2_words, 0, 512)
-        load_scales(ys2, 0, y2_scales)
-        load_words(xw1, x1_words, 512, 1024)
-        load_words(xw2, x2_words, 512, 1024)
+        nc.gpsimd.dma_start(out=xsc[:].rearrange("p (g t) -> p g t", t=4), in_=x_scale.rearrange("o (g p t) -> p (o g) t", p=P, t=4))
+        ident_f = keep.tile([P, P], F32, align_bytes=256, name="ident_f")
+        make_identity(nc, ident_f[:])
+        ident_b = keep.tile([P, P], BF16, align_bytes=256, name="ident_b")
+        make_identity(nc, ident_b[:])
+        nc.gpsimd.dma_start(out=gn[:].rearrange("p (g t) -> p g t", t=4), in_=gain.rearrange("(g p t) -> p g t", p=P, t=4))
+        sc = {"a": (xs, 0, x1_scales), "b": (xs, 4, x2_scales), "c": (ys1, 0, y1_scales), "d": (ys2, 0, y2_scales)}
+        wd = {"A": (xw1, x1_words), "B": (xw2, x2_words), "C": (yw1, y1_words), "D": (yw2, y2_words)}
+        for token in ORDER.split():
+            if token in sc:
+                load_scales(*sc[token])
+            elif token[0] in wd:
+                load_words(*wd[token[0]], 512 * int(token[1]), 512 * int(token[1]) + 512)
+            else:
+                load_x(int(token[0]), int(token[1]))
         w0t = keep.tile([P, 8, 1024], BF16, align_bytes=256, name="w0t")
         w0_rows = w0.rearrange("(g p t) f -> g p t f", p=P, t=4)
         for h in range(2):
@@ -113,7 +108,6 @@ def tile_fedparatanhhadamardlinear_w8_kernel(
                 out=diag[:, i, :], in0=ident_b[:], scalar1=gn[:, i : i + 1], scalar2=0.0, op0=ALU.mult, op1=ALU.add,
             )
         g01 = keep.tile([P, 8], F32, name="g01")
-        nc.vector.tensor_scalar(out=g01[:], in0=gn[:], scalar1=0.1, scalar2=None, op0=ALU.mult)
 
         xg = keep.tile([P, 2, 4096], BF16, align_bytes=256, name="xg")
         xq = keep.tile([P, 2, 1024], U32, align_bytes=256, name="xq")
@@ -122,8 +116,11 @@ def tile_fedparatanhhadamardlinear_w8_kernel(
 
         def cast(rt):
             tile_f = xio.tile([P, 1024], BF16, align_bytes=256, name="xf")
-            src = xb[rt // 2][:, rt % 2, :].bitcast(FP8)
-            if CAST[rt] == "s":
+            src = xb[:, rt, :].bitcast(FP8)
+            if CAST[rt] == "h":
+                for g in range(2):
+                    nc.scalar.copy(out=tile_f[:, 512 * g : 512 * g + 512], in_=src[:, 512 * g : 512 * g + 512])
+            elif CAST[rt] == "s":
                 nc.scalar.copy(out=tile_f[:], in_=src)
             elif CAST[rt] == "v":
                 nc.vector.tensor_copy(out=tile_f[:], in_=src)
@@ -159,9 +156,10 @@ def tile_fedparatanhhadamardlinear_w8_kernel(
         xsp = keep.tile([P, 1024], U8, align_bytes=256, name="xsp")
 
         def perm(eng, dst, src, dtype, g):
+            run = 4 if dtype == I32 else 16
             eng.tensor_copy(
-                out=dst[:, 512 * g : 512 * g + 512].bitcast(dtype).rearrange("p (t m) -> p t m", t=4),
-                in_=src[:, 512 * g : 512 * g + 512].bitcast(dtype).rearrange("p (m t) -> p t m", t=4),
+                out=dst[:, 512 * g : 512 * g + 512].bitcast(dtype).rearrange("p (t c i) -> p c t i", t=4, i=run),
+                in_=src[:, 512 * g : 512 * g + 512].bitcast(dtype).rearrange("p (c i t) -> p c t i", t=4, i=run),
             )
 
         wq = keep.tile([P, 2, 1024], U32, align_bytes=256, name="wq")
@@ -189,23 +187,30 @@ def tile_fedparatanhhadamardlinear_w8_kernel(
             nc.scalar.activation(out=s2[:], in_=b2[:], func=ACT.Sigmoid, scale=2.0)
             return t1, s2
 
-        def product(u, t1, s2, g, ts, w, on_g):
+        def product(u, t1, s2, g, ts, w):
             for j, t in enumerate(ts):
-                if on_g:
-                    nc.gpsimd.tensor_scalar(
-                        out=t1[:, j * w : j * w + w], in0=t1[:, j * w : j * w + w], scalar1=g01[:, 4 * g + t : 4 * g + t + 1],
-                        scalar2=0.0, op0=ALU.mult, op1=ALU.add,
-                    )
-                    nc.gpsimd.tensor_tensor(
-                        out=u[:, t, :], in0=t1[:, j * w : j * w + w], in1=s2[:, j * w : j * w + w], op=ALU.mult,
-                    )
-                    continue
                 nc.vector.scalar_tensor_tensor(
                     out=u[:, t, :], in0=t1[:, j * w : j * w + w], scalar=g01[:, 4 * g + t : 4 * g + t + 1],
                     in1=s2[:, j * w : j * w + w], op0=ALU.mult, op1=ALU.mult,
                 )
 
         banks = {}
+
+        def sum_on_pe(wb, u, g, f0, fb):
+            bank = ps_xo.tile([P, BANK], F32, name="xo")
+            for t in range(4):
+                cols = slice(128 * t, 128 * t + 128)
+                nc.tensor.matmul(
+                    out=bank[:, cols], lhsT=diag[:, 4 * g + t, :],
+                    rhs=w0t[:, 4 * g + t, f0 + 128 * fb : f0 + 128 * fb + 128], start=True, stop=False,
+                )
+                nc.tensor.matmul(
+                    out=bank[:, cols], lhsT=ident_f[:], rhs=u[:, t, 128 * fb : 128 * fb + 128], start=False, stop=True,
+                )
+            nc.scalar.copy(
+                out=wb[:, 512 * fb : 512 * fb + 512].rearrange("p (f t) -> p f t", t=4),
+                in_=bank[:].rearrange("p (t f) -> p f t", t=4),
+            )
 
         def base_bank(g, f0, fb):
             bank = ps_gw.tile([P, BANK], F32, name="gw")
@@ -227,8 +232,8 @@ def tile_fedparatanhhadamardlinear_w8_kernel(
         def w_quant(wb, g, f0, w):
             nc.vector.quantize_mx(out=wq[:, g, f0 : f0 + w].bitcast(FP8X4), scales=wqs[:, g, f0 : f0 + w], in_=wb[:])
 
-        def main(f0, w, b):
-            n_t = BANK // w
+        def main(f0, w, n_t, b, on_vector):
+            size = n_t * w
             bank = ps_xo.tile([P, BANK], F32, name="xo")
             for j in range(n_t):
                 rows = slice(128 * (b * n_t + j), 128 * (b * n_t + j) + 128)
@@ -239,12 +244,12 @@ def tile_fedparatanhhadamardlinear_w8_kernel(
                         start=(g == 0), stop=(g == 1),
                     )
             o = outs.tile([P, BANK], F32, name="o")
-            if (f0 + w == F and b % 2 == 1) or b < OUTV:
-                nc.vector.tensor_copy(out=o[:], in_=bank[:])
+            if on_vector:
+                nc.vector.tensor_copy(out=o[:, :size], in_=bank[:, :size])
             else:
-                nc.scalar.copy(out=o[:], in_=bank[:])
+                nc.scalar.copy(out=o[:, :size], in_=bank[:, :size])
             nc.sync.dma_start(
-                out=out_rows[:, b * n_t : b * n_t + n_t, f0 : f0 + w], in_=o[:].rearrange("p (j w) -> p j w", w=w),
+                out=out_rows[:, b * n_t : b * n_t + n_t, f0 : f0 + w], in_=o[:, :size].rearrange("p (j w) -> p j w", w=w),
             )
 
         ctx.enter_context(tc.manual_schedule(engines={mybir.EngineType.DVE}))
@@ -274,7 +279,7 @@ def tile_fedparatanhhadamardlinear_w8_kernel(
                 wb = upd.tile([P, 4 * w], BF16, align_bytes=256, name="wb")
                 tiles[(f0, g)] = (u, wb)
             t1, s2 = made[len(used)]
-            product(tiles[(f0, g)][0], t1, s2, g, ts, w, False)
+            product(tiles[(f0, g)][0], t1, s2, g, ts, w)
             used.append(1)
 
         mq = []
@@ -282,8 +287,10 @@ def tile_fedparatanhhadamardlinear_w8_kernel(
         def seal(f0, w, g):
             w_quant(tiles[(f0, g)][1], g, f0, w)
             if g == 1:
-                for b in range(8 * w // BANK):
-                    mq.append(lambda b=b: main(f0, w, b))
+                last = f0 + w == F
+                n_t = LAST_T if last else BANK // w
+                for b in range(8 // n_t):
+                    mq.append(lambda b=b: main(f0, w, n_t, b, last and b % 2 == 1))
 
         def weave(a, b):
             res = []
@@ -298,9 +305,8 @@ def tile_fedparatanhhadamardlinear_w8_kernel(
             return (run, ahead)
 
         def x_task(rp, g):
-            if g == 0:
-                cast(2 * rp)
-                cast(2 * rp + 1)
+            for rt in range(len(xf), min(8, 2 * rp + 2 + CASTS_AHEAD * (g + 1))):
+                cast(rt)
             x_turn(rp, g)
 
         def perm_task(dst, src, dtype, g):
@@ -311,21 +317,26 @@ def tile_fedparatanhhadamardlinear_w8_kernel(
             perm_task(dst, src, dtype, g) for g in range(2)
             for dst, src, dtype in ((xsp, xs, U8), (x1p, xw1, I32), (x2p, xw2, I32))
         ]
-        seq = turns[:XSPLIT] + perms[:3] + turns[XSPLIT:6] + perms[3:] + [task(lambda g=g: x_quant(0, g)) for g in range(2)]
-        rest = turns[6:] + [task(lambda g=g: x_quant(1, g)) for g in range(2)]
+        gains = [task(lambda: nc.vector.tensor_scalar(out=g01[:], in0=gn[:], scalar1=0.1, scalar2=None, op0=ALU.mult))]
+        seq = turns[:PERM_AT[0]] + perms[:3] + turns[PERM_AT[0]:PERM_AT[1]] + perms[3:] + turns[PERM_AT[1]:XHEAD] + [task(lambda g=g: x_quant(0, g)) for g in range(2)] + gains
+        rest = turns[XHEAD:] + [task(lambda g=g: x_quant(1, g)) for g in range(2)]
         carry = []
         for phase in units:
             seq += weave([task(product_next) for a in phase], rest)
             g, ts, f0, w = phase[0]
+            on_pe = len([1 for key in SUM_PE if key == (f0, g)])
             rest = carry + [
+                task(lambda fb=fb, f0=f0, g=g: sum_on_pe(tiles[(f0, g)][1], tiles[(f0, g)][0], g, f0, fb))
+                for fb in range(on_pe)
+            ] + [
                 task(
                     lambda fb=fb, f0=f0, g=g: add_base(tiles[(f0, g)][1], tiles[(f0, g)][0], g, f0, fb),
                     lambda fb=fb, f0=f0, g=g: base_bank(g, f0, fb),
                 )
-                for fb in range(w // 128)
+                for fb in range(on_pe, w // 128)
             ]
             carry = [task(lambda w=w, f0=f0, g=g: seal(f0, w, g))]
-        seq += rest + carry
+        seq += rest[1:] + rest[:1] + carry
         ahead = [(i, a) for i, (run, a) in enumerate(seq) if a]
         for i, (run, a) in enumerate(seq):
             while ahead and ahead[0][0] <= i + AHEAD:

@@ -20,13 +20,15 @@ P = 128
 BANK = 512
 WIDTHS = (512, 256, 128, 128)
 CAST = ("v", "h", "s", "s", "s", "s", "s", "s")
-LEAD = 5
+LEAD = 3
+TANH_LEAD = 2
 AHEAD = 2
-CASTS_AHEAD = 0
+CASTS_AHEAD = 2
 NMQ = 1
 LAST_T = 2
-ORDER = "02 24 a 48 A0 C0 c b B0 D0 d A1 B1"
-PERM_AT = (4, 6)
+OUT_V = ()
+ORDER = "02 24 48 a A0 C0 c b B0 D0 d A1 B1"
+PERM_AT = (5, 7)
 XHEAD = 6
 SUM_PE = ((0, 0), (0, 1))
 PERM_G = "vvvv"
@@ -40,7 +42,7 @@ def tile_fedparatanhhadamardlinear_w8_kernel(
     with ExitStack() as ctx:
         keep = ctx.enter_context(tc.tile_pool(name="keep", bufs=1))
         xio = ctx.enter_context(tc.tile_pool(name="xio", bufs=8))
-        acts = ctx.enter_context(tc.tile_pool(name="acts", bufs=8))
+        acts = ctx.enter_context(tc.tile_pool(name="acts", bufs=12))
         upd = ctx.enter_context(tc.tile_pool(name="upd", bufs=3))
         outs = ctx.enter_context(tc.tile_pool(name="outs", bufs=10))
         ps_p = ctx.enter_context(tc.psum_pool(name="ps_p", bufs=3))
@@ -48,11 +50,12 @@ def tile_fedparatanhhadamardlinear_w8_kernel(
         ps_xo = ctx.enter_context(tc.psum_pool(name="ps_xo", bufs=3))
 
         scale_tiles = []
-        for i in range(3):
+        for i in range(4):
             tile_s = keep.tile([P, 1024], U8, align_bytes=256, name="sc%d" % i)
-            nc.vector.memset(tile_s[:].bitcast(I32), 0)
+            eng = nc.gpsimd if i == 0 else nc.vector
+            eng.memset(tile_s[:].bitcast(I32), 0)
             scale_tiles.append(tile_s)
-        xs, ys1, ys2 = scale_tiles
+        xs1, xs2, ys1, ys2 = scale_tiles
         warm = keep.tile([P, 1], F32, name="warm")
         warm_out = keep.tile([P, 1], F32, name="warm_out")
         nc.vector.memset(warm[:], 0.0)
@@ -78,13 +81,13 @@ def tile_fedparatanhhadamardlinear_w8_kernel(
 
         gn = keep.tile([P, 8], BF16, name="gn")
         xsc = keep.tile([P, 8], F32, name="xsc")
-        nc.gpsimd.dma_start(out=xsc[:].rearrange("p (g t) -> p g t", t=4), in_=x_scale.rearrange("o (g p t) -> p (o g) t", p=P, t=4))
+        nc.scalar.dma_start(out=xsc[:].rearrange("p (g t) -> p g t", t=4), in_=x_scale.rearrange("o (g p t) -> p (o g) t", p=P, t=4))
         ident_f = keep.tile([P, P], F32, align_bytes=256, name="ident_f")
         make_identity(nc, ident_f[:])
         ident_b = keep.tile([P, P], BF16, align_bytes=256, name="ident_b")
         make_identity(nc, ident_b[:])
         nc.gpsimd.dma_start(out=gn[:].rearrange("p (g t) -> p g t", t=4), in_=gain.rearrange("(g p t) -> p g t", p=P, t=4))
-        sc = {"a": (xs, 0, x1_scales), "b": (xs, 4, x2_scales), "c": (ys1, 0, y1_scales), "d": (ys2, 0, y2_scales)}
+        sc = {"a": (xs1, 0, x1_scales), "b": (xs2, 0, x2_scales), "c": (ys1, 0, y1_scales), "d": (ys2, 0, y2_scales)}
         wd = {"A": (xw1, x1_words), "B": (xw2, x2_words), "C": (yw1, y1_words), "D": (yw2, y2_words)}
         for token in ORDER.split():
             if token in sc:
@@ -153,7 +156,10 @@ def tile_fedparatanhhadamardlinear_w8_kernel(
 
         x1p = keep.tile([P, 1024], U32, align_bytes=256, name="x1p")
         x2p = keep.tile([P, 1024], U32, align_bytes=256, name="x2p")
-        xsp = keep.tile([P, 1024], U8, align_bytes=256, name="xsp")
+        xsp1 = keep.tile([P, 1024], U8, align_bytes=256, name="xsp1")
+        xsp2 = keep.tile([P, 1024], U8, align_bytes=256, name="xsp2")
+
+        halves = ((x1p, xsp1, yw1, ys1), (x2p, xsp2, yw2, ys2))
 
         def perm(eng, dst, src, dtype, g):
             run = 4 if dtype == I32 else 16
@@ -166,26 +172,22 @@ def tile_fedparatanhhadamardlinear_w8_kernel(
         wqs = keep.tile([P, 2, 1024], U8, align_bytes=256, name="wqs")
         out_rows = out.rearrange("(r p) f -> p r f", p=P)
 
-        def unit(g, ts, f0, w):
-            b1 = ps_p.tile([P, BANK], F32, name="pbank")
+        def factor(half, g, ts, f0, w):
+            xp, xsp, yw, ys = halves[half]
+            bank = ps_p.tile([P, BANK], F32, name="pbank")
             for j, t in enumerate(ts):
                 st = slice(512 * g + 128 * t, 512 * g + 128 * t + 128)
                 nc.tensor.matmul_mx(
-                    out=b1[:, j * w : j * w + w], lhsT=x1p[:, st].bitcast(FP8X4), lhsT_scale=xsp[:, st],
-                    rhs=yw1[:, f0 : f0 + w].bitcast(FP8X4), rhs_scale=ys1[:, f0 : f0 + w], start=True, stop=True,
+                    out=bank[:, j * w : j * w + w], lhsT=xp[:, st].bitcast(FP8X4), lhsT_scale=xsp[:, st],
+                    rhs=yw[:, f0 : f0 + w].bitcast(FP8X4), rhs_scale=ys[:, f0 : f0 + w], start=True, stop=True,
                 )
-            t1 = acts.tile([P, BANK], F32, name="t1")
-            nc.scalar.activation(out=t1[:], in_=b1[:], func=ACT.Tanh)
-            b2 = ps_p.tile([P, BANK], F32, name="pbank")
-            for j, t in enumerate(ts):
-                st = slice(512 * g + 128 * t, 512 * g + 128 * t + 128)
-                nc.tensor.matmul_mx(
-                    out=b2[:, j * w : j * w + w], lhsT=x2p[:, st].bitcast(FP8X4), lhsT_scale=xsp[4:P, st],
-                    rhs=yw2[:, f0 : f0 + w].bitcast(FP8X4), rhs_scale=ys2[:, f0 : f0 + w], start=True, stop=True,
-                )
-            s2 = acts.tile([P, BANK], F32, name="s2")
-            nc.scalar.activation(out=s2[:], in_=b2[:], func=ACT.Sigmoid, scale=2.0)
-            return t1, s2
+            if half == 0:
+                res = acts.tile([P, BANK], F32, name="t1")
+                nc.scalar.activation(out=res[:], in_=bank[:], func=ACT.Tanh)
+            else:
+                res = acts.tile([P, BANK], F32, name="s2")
+                nc.scalar.activation(out=res[:], in_=bank[:], func=ACT.Sigmoid, scale=2.0)
+            return res
 
         def product(u, t1, s2, g, ts, w):
             for j, t in enumerate(ts):
@@ -265,9 +267,19 @@ def tile_fedparatanhhadamardlinear_w8_kernel(
         flat = [a for phase in units for a in phase]
         tiles = {}
 
+        tanhs = []
+
+        second = []
+
         def make_units(upto):
             while len(made) < min(upto, len(flat)):
-                made.append(unit(*flat[len(made)]))
+                if len(made) + TANH_LEAD >= 4 and not second:
+                    second.extend(perms[2] + perms[3])
+                    for run, ahead_of in second:
+                        run()
+                while len(tanhs) < min(len(flat), len(made) + 1 + TANH_LEAD):
+                    tanhs.append(factor(0, *flat[len(tanhs)]))
+                made.append(factor(1, *flat[len(made)]))
 
         used = []
 
@@ -278,7 +290,7 @@ def tile_fedparatanhhadamardlinear_w8_kernel(
                 u = upd.tile([P, 4, w], F32, align_bytes=256, name="u")
                 wb = upd.tile([P, 4 * w], BF16, align_bytes=256, name="wb")
                 tiles[(f0, g)] = (u, wb)
-            t1, s2 = made[len(used)]
+            t1, s2 = tanhs[len(used)], made[len(used)]
             product(tiles[(f0, g)][0], t1, s2, g, ts, w)
             used.append(1)
 
@@ -290,7 +302,7 @@ def tile_fedparatanhhadamardlinear_w8_kernel(
                 last = f0 + w == F
                 n_t = LAST_T if last else BANK // w
                 for b in range(8 // n_t):
-                    mq.append(lambda b=b: main(f0, w, n_t, b, last and b % 2 == 1))
+                    mq.append(lambda b=b: main(f0, w, n_t, b, (last and b % 2 == 1) or (f0, b) in OUT_V))
 
         def weave(a, b):
             res = []
@@ -314,11 +326,18 @@ def tile_fedparatanhhadamardlinear_w8_kernel(
 
         turns = [task(lambda rp=rp, g=g: x_task(rp, g)) for rp in range(4) for g in range(2)]
         perms = [
-            perm_task(dst, src, dtype, g) for g in range(2)
-            for dst, src, dtype in ((xsp, xs, U8), (x1p, xw1, I32), (x2p, xw2, I32))
+            [perm_task(xsp1, xs1, U8, g), perm_task(x1p, xw1, I32, g)] if one
+            else [perm_task(xsp2, xs2, U8, g), perm_task(x2p, xw2, I32, g)]
+            for g in range(2) for one in (True, False)
         ]
         gains = [task(lambda: nc.vector.tensor_scalar(out=g01[:], in0=gn[:], scalar1=0.1, scalar2=None, op0=ALU.mult))]
-        seq = turns[:PERM_AT[0]] + perms[:3] + turns[PERM_AT[0]:PERM_AT[1]] + perms[3:] + turns[PERM_AT[1]:XHEAD] + [task(lambda g=g: x_quant(0, g)) for g in range(2)] + gains
+        head = turns[:XHEAD] + [task(lambda g=g: x_quant(0, g)) for g in range(2)] + gains
+        seq = []
+        for i in range(len(head) + 1):
+            for j in range(2):
+                if PERM_AT[j] == i:
+                    seq += perms[j]
+            seq += head[i:i + 1]
         rest = turns[XHEAD:] + [task(lambda g=g: x_quant(1, g)) for g in range(2)]
         carry = []
         for phase in units:

from contextlib import ExitStack

import concourse.mybir as mybir
from concourse.masks import make_identity

T, D, F, R = 1024, 1024, 1024, 512
FLOPS = 2 * D * F * R * 2 + 2 * T * D * F

F32 = mybir.dt.float32
BF16 = mybir.dt.bfloat16
I32 = mybir.dt.int32
U32 = mybir.dt.uint32
U8 = mybir.dt.uint8
FP8 = mybir.dt.float8_e4m3fn
FP8X4 = mybir.dt.float8_e4m3fn_x4
ACT = mybir.ActivationFunctionType
ALU = mybir.AluOpType

P = 128
BANK = 512
WIDTHS = (512, 256, 128, 128)
CAST = ("v", "h", "s", "s", "s", "s", "s", "s")
LEAD = 3
TANH_LEAD = 2
AHEAD = 2
CASTS_AHEAD = 2
NMQ = 1
LAST_T = 2
OUT_V = ()
ORDER = "02 24 48 a A0 C0 c b B0 D0 d A1 B1"
PERM_AT = (5, 7)
XHEAD = 6
SUM_PE = ((0, 0), (0, 1))
PERM_G = "vvvv"


def tile_fedparatanhhadamardlinear_w8_kernel(
    tc, x_bytes, x_scale, w0, x1_words, x1_scales, y1_words, y1_scales,
    x2_words, x2_scales, y2_words, y2_scales, gain, out,
):
    nc = tc.nc
    with ExitStack() as ctx:
        keep = ctx.enter_context(tc.tile_pool(name="keep", bufs=1))
        xio = ctx.enter_context(tc.tile_pool(name="xio", bufs=8))
        acts = ctx.enter_context(tc.tile_pool(name="acts", bufs=12))
        upd = ctx.enter_context(tc.tile_pool(name="upd", bufs=3))
        outs = ctx.enter_context(tc.tile_pool(name="outs", bufs=10))
        ps_p = ctx.enter_context(tc.psum_pool(name="ps_p", bufs=3))
        ps_gw = ctx.enter_context(tc.psum_pool(name="ps_gw", bufs=2))
        ps_xo = ctx.enter_context(tc.psum_pool(name="ps_xo", bufs=3))

        scale_tiles = []
        for i in range(4):
            tile_s = keep.tile([P, 1024], U8, align_bytes=256, name="sc%d" % i)
            eng = nc.gpsimd if i == 0 else nc.vector
            eng.memset(tile_s[:].bitcast(I32), 0)
            scale_tiles.append(tile_s)
        xs1, xs2, ys1, ys2 = scale_tiles
        warm = keep.tile([P, 1], F32, name="warm")
        warm_out = keep.tile([P, 1], F32, name="warm_out")
        nc.vector.memset(warm[:], 0.0)
        nc.scalar.activation(out=warm_out[:], in_=warm[:], func=ACT.Sigmoid)

        x_rows = x_bytes.rearrange("(r p) k -> p r k", p=P)
        xb = keep.tile([P, 8, 1024], U8, align_bytes=256, name="xb")
        xw1 = keep.tile([P, 1024], U32, align_bytes=256, name="xw1")
        xw2 = keep.tile([P, 1024], U32, align_bytes=256, name="xw2")
        yw1 = keep.tile([P, 1024], U32, align_bytes=256, name="yw1")
        yw2 = keep.tile([P, 1024], U32, align_bytes=256, name="yw2")

        def load_x(r0, r1):
            nc.sync.dma_start(out=xb[:, r0:r1, :], in_=x_rows[:, r0:r1, :])

        def load_scales(tile_s, k, scales):
            for r in range(4):
                nc.sync.dma_start(out=tile_s[k + r : P : 32, :].bitcast(I32), in_=scales[0, r:16:4, :].bitcast(I32))

        def load_words(tile_w, words, c0, c1):
            flat = words[0].rearrange("p n t -> p (n t)")
            nc.sync.dma_start(out=tile_w[:, c0:c1].bitcast(I32), in_=flat[:, 4 * c0 : 4 * c1].bitcast(I32))

        gn = keep.tile([P, 8], BF16, name="gn")
        xsc = keep.tile([P, 8], F32, name="xsc")
        nc.scalar.dma_start(out=xsc[:].rearrange("p (g t) -> p g t", t=4), in_=x_scale.rearrange("o (g p t) -> p (o g) t", p=P, t=4))
        ident_f = keep.tile([P, P], F32, align_bytes=256, name="ident_f")
        make_identity(nc, ident_f[:])
        ident_b = keep.tile([P, P], BF16, align_bytes=256, name="ident_b")
        make_identity(nc, ident_b[:])
        nc.gpsimd.dma_start(out=gn[:].rearrange("p (g t) -> p g t", t=4), in_=gain.rearrange("(g p t) -> p g t", p=P, t=4))
        sc = {"a": (xs1, 0, x1_scales), "b": (xs2, 0, x2_scales), "c": (ys1, 0, y1_scales), "d": (ys2, 0, y2_scales)}
        wd = {"A": (xw1, x1_words), "B": (xw2, x2_words), "C": (yw1, y1_words), "D": (yw2, y2_words)}
        for token in ORDER.split():
            if token in sc:
                load_scales(*sc[token])
            elif token[0] in wd:
                load_words(*wd[token[0]], 512 * int(token[1]), 512 * int(token[1]) + 512)
            else:
                load_x(int(token[0]), int(token[1]))
        w0t = keep.tile([P, 8, 1024], BF16, align_bytes=256, name="w0t")
        w0_rows = w0.rearrange("(g p t) f -> g p t f", p=P, t=4)
        for h in range(2):
            for g in range(2):
                nc.sync.dma_start(out=w0t[:, 4 * g : 4 * g + 4, 512 * h : 512 * h + 512], in_=w0_rows[g][:, :, 512 * h : 512 * h + 512])
            if h == 0:
                load_words(yw1, y1_words, 512, 1024)
                load_words(yw2, y2_words, 512, 1024)

        diag = keep.tile([P, 8, P], BF16, align_bytes=256, name="diag")
        for i in range(8):
            nc.gpsimd.tensor_scalar(
                out=diag[:, i, :], in0=ident_b[:], scalar1=gn[:, i : i + 1], scalar2=0.0, op0=ALU.mult, op1=ALU.add,
            )
        g01 = keep.tile([P, 8], F32, name="g01")

        xg = keep.tile([P, 2, 4096], BF16, align_bytes=256, name="xg")
        xq = keep.tile([P, 2, 1024], U32, align_bytes=256, name="xq")
        xqs = keep.tile([P, 2, 1024], U8, align_bytes=256, name="xqs")
        xf = {}

        def cast(rt):
            tile_f = xio.tile([P, 1024], BF16, align_bytes=256, name="xf")
            src = xb[:, rt, :].bitcast(FP8)
            if CAST[rt] == "h":
                for g in range(2):
                    nc.scalar.copy(out=tile_f[:, 512 * g : 512 * g + 512], in_=src[:, 512 * g : 512 * g + 512])
            elif CAST[rt] == "s":
                nc.scalar.copy(out=tile_f[:], in_=src)
            elif CAST[rt] == "v":
                nc.vector.tensor_copy(out=tile_f[:], in_=src)
            else:
                nc.gpsimd.tensor_copy(out=tile_f[:], in_=src)
            xf[rt] = tile_f

        def x_turn(rp, g):
            bank = ps_xo.tile([P, BANK], F32, name="xo")
            for r2 in range(2):
                words = xf[2 * rp + r2][:].bitcast(F32)
                for u in range(2):
                    nc.tensor.transpose(
                        bank[:, 256 * u + 128 * r2 : 256 * u + 128 * r2 + 128],
                        words[:, 256 * g + u : 256 * (g + 1) : 2], ident_f[:],
                    )
            nc.vector.tensor_tensor(
                out=xg[:, g, 1024 * rp : 1024 * rp + 1024].rearrange("p (r u e) -> p r u e", u=2, e=2),
                in0=bank[:].bitcast(BF16).rearrange("p (u r e) -> p r u e", u=2, e=2),
                in1=xsc[:, 4 * g : 4 * g + 4].rearrange("p (u e) -> p u e", e=2).unsqueeze(1).to_broadcast([P, 256, 2, 2]),
                op=ALU.mult,
            )

        def x_quant(half, g):
            cols = slice(512 * half, 512 * half + 512)
            nc.vector.quantize_mx(
                out=xq[:, g, cols].bitcast(FP8X4), scales=xqs[:, g, cols],
                in_=xg[:, g, 2048 * half : 2048 * half + 2048],
            )

        x1p = keep.tile([P, 1024], U32, align_bytes=256, name="x1p")
        x2p = keep.tile([P, 1024], U32, align_bytes=256, name="x2p")
        xsp1 = keep.tile([P, 1024], U8, align_bytes=256, name="xsp1")
        xsp2 = keep.tile([P, 1024], U8, align_bytes=256, name="xsp2")

        halves = ((x1p, xsp1, yw1, ys1), (x2p, xsp2, yw2, ys2))

        def perm(eng, dst, src, dtype, g):
            run = 4 if dtype == I32 else 16
            eng.tensor_copy(
                out=dst[:, 512 * g : 512 * g + 512].bitcast(dtype).rearrange("p (t c i) -> p c t i", t=4, i=run),
                in_=src[:, 512 * g : 512 * g + 512].bitcast(dtype).rearrange("p (c i t) -> p c t i", t=4, i=run),
            )

        wq = keep.tile([P, 2, 1024], U32, align_bytes=256, name="wq")
        wqs = keep.tile([P, 2, 1024], U8, align_bytes=256, name="wqs")
        out_rows = out.rearrange("(r p) f -> p r f", p=P)

        def factor(half, g, ts, f0, w):
            xp, xsp, yw, ys = halves[half]
            bank = ps_p.tile([P, BANK], F32, name="pbank")
            for j, t in enumerate(ts):
                st = slice(512 * g + 128 * t, 512 * g + 128 * t + 128)
                nc.tensor.matmul_mx(
                    out=bank[:, j * w : j * w + w], lhsT=xp[:, st].bitcast(FP8X4), lhsT_scale=xsp[:, st],
                    rhs=yw[:, f0 : f0 + w].bitcast(FP8X4), rhs_scale=ys[:, f0 : f0 + w], start=True, stop=True,
                )
            if half == 0:
                res = acts.tile([P, BANK], F32, name="t1")
                nc.scalar.activation(out=res[:], in_=bank[:], func=ACT.Tanh)
            else:
                res = acts.tile([P, BANK], F32, name="s2")
                nc.scalar.activation(out=res[:], in_=bank[:], func=ACT.Sigmoid, scale=2.0)
            return res

        def product(u, t1, s2, g, ts, w):
            for j, t in enumerate(ts):
                nc.vector.scalar_tensor_tensor(
                    out=u[:, t, :], in0=t1[:, j * w : j * w + w], scalar=g01[:, 4 * g + t : 4 * g + t + 1],
                    in1=s2[:, j * w : j * w + w], op0=ALU.mult, op1=ALU.mult,
                )

        banks = {}

        def sum_on_pe(wb, u, g, f0, fb):
            bank = ps_xo.tile([P, BANK], F32, name="xo")
            for t in range(4):
                cols = slice(128 * t, 128 * t + 128)
                nc.tensor.matmul(
                    out=bank[:, cols], lhsT=diag[:, 4 * g + t, :],
                    rhs=w0t[:, 4 * g + t, f0 + 128 * fb : f0 + 128 * fb + 128], start=True, stop=False,
                )
                nc.tensor.matmul(
                    out=bank[:, cols], lhsT=ident_f[:], rhs=u[:, t, 128 * fb : 128 * fb + 128], start=False, stop=True,
                )
            nc.scalar.copy(
                out=wb[:, 512 * fb : 512 * fb + 512].rearrange("p (f t) -> p f t", t=4),
                in_=bank[:].rearrange("p (t f) -> p f t", t=4),
            )

        def base_bank(g, f0, fb):
            bank = ps_gw.tile([P, BANK], F32, name="gw")
            for t in range(4):
                nc.tensor.matmul(
                    out=bank[:, 128 * t : 128 * t + 128], lhsT=diag[:, 4 * g + t, :],
                    rhs=w0t[:, 4 * g + t, f0 + 128 * fb : f0 + 128 * fb + 128], start=True, stop=True,
                )
            banks[(g, f0, fb)] = bank

        def add_base(wb, u, g, f0, fb):
            bank = banks[(g, f0, fb)]
            nc.vector.tensor_tensor(
                out=wb[:, 512 * fb : 512 * fb + 512].rearrange("p (c i t) -> p c t i", i=4, t=4),
                in0=bank[:].rearrange("p (t c i) -> p c t i", t=4, i=4),
                in1=u[:, :, 128 * fb : 128 * fb + 128].rearrange("p t (c i) -> p c t i", i=4), op=ALU.add,
            )

        def w_quant(wb, g, f0, w):
            nc.vector.quantize_mx(out=wq[:, g, f0 : f0 + w].bitcast(FP8X4), scales=wqs[:, g, f0 : f0 + w], in_=wb[:])

        def main(f0, w, n_t, b, on_vector):
            size = n_t * w
            bank = ps_xo.tile([P, BANK], F32, name="xo")
            for j in range(n_t):
                rows = slice(128 * (b * n_t + j), 128 * (b * n_t + j) + 128)
                for g in range(2):
                    nc.tensor.matmul_mx(
                        out=bank[:, j * w : j * w + w], lhsT=xq[:, g, rows].bitcast(FP8X4), lhsT_scale=xqs[:, g, rows],
                        rhs=wq[:, g, f0 : f0 + w].bitcast(FP8X4), rhs_scale=wqs[:, g, f0 : f0 + w],
                        start=(g == 0), stop=(g == 1),
                    )
            o = outs.tile([P, BANK], F32, name="o")
            if on_vector:
                nc.vector.tensor_copy(out=o[:, :size], in_=bank[:, :size])
            else:
                nc.scalar.copy(out=o[:, :size], in_=bank[:, :size])
            nc.sync.dma_start(
                out=out_rows[:, b * n_t : b * n_t + n_t, f0 : f0 + w], in_=o[:, :size].rearrange("p (j w) -> p j w", w=w),
            )

        ctx.enter_context(tc.manual_schedule(engines={mybir.EngineType.DVE}))
        units = []
        f0 = 0
        for w in WIDTHS:
            n_t = BANK // w
            for g in range(2):
                units.append([(g, list(range(k * n_t, k * n_t + n_t)), f0, w) for k in range(4 // n_t)])
            f0 += w

        made = []
        flat = [a for phase in units for a in phase]
        tiles = {}

        tanhs = []

        second = []

        def make_units(upto):
            while len(made) < min(upto, len(flat)):
                if len(made) + TANH_LEAD >= 4 and not second:
                    second.extend(perms[2] + perms[3])
                    for run, ahead_of in second:
                        run()
                while len(tanhs) < min(len(flat), len(made) + 1 + TANH_LEAD):
                    tanhs.append(factor(0, *flat[len(tanhs)]))
                made.append(factor(1, *flat[len(made)]))

        used = []

        def product_next():
            g, ts, f0, w = flat[len(used)]
            make_units(len(used) + 1 + LEAD)
            if ts[0] == 0:
                u = upd.tile([P, 4, w], F32, align_bytes=256, name="u")
                wb = upd.tile([P, 4 * w], BF16, align_bytes=256, name="wb")
                tiles[(f0, g)] = (u, wb)
            t1, s2 = tanhs[len(used)], made[len(used)]
            product(tiles[(f0, g)][0], t1, s2, g, ts, w)
            used.append(1)

        mq = []

        def seal(f0, w, g):
            w_quant(tiles[(f0, g)][1], g, f0, w)
            if g == 1:
                last = f0 + w == F
                n_t = LAST_T if last else BANK // w
                for b in range(8 // n_t):
                    mq.append(lambda b=b: main(f0, w, n_t, b, (last and b % 2 == 1) or (f0, b) in OUT_V))

        def weave(a, b):
            res = []
            for i in range(max(len(a), len(b))):
                if i < len(a):
                    res.append(a[i])
                if i < len(b):
                    res.append(b[i])
            return res

        def task(run, ahead=None):
            return (run, ahead)

        def x_task(rp, g):
            for rt in range(len(xf), min(8, 2 * rp + 2 + CASTS_AHEAD * (g + 1))):
                cast(rt)
            x_turn(rp, g)

        def perm_task(dst, src, dtype, g):
            return task(lambda: perm(nc.vector, dst, src, dtype, g))

        turns = [task(lambda rp=rp, g=g: x_task(rp, g)) for rp in range(4) for g in range(2)]
        perms = [
            [perm_task(xsp1, xs1, U8, g), perm_task(x1p, xw1, I32, g)] if one
            else [perm_task(xsp2, xs2, U8, g), perm_task(x2p, xw2, I32, g)]
            for g in range(2) for one in (True, False)
        ]
        gains = [task(lambda: nc.vector.tensor_scalar(out=g01[:], in0=gn[:], scalar1=0.1, scalar2=None, op0=ALU.mult))]
        head = turns[:XHEAD] + [task(lambda g=g: x_quant(0, g)) for g in range(2)] + gains
        seq = []
        for i in range(len(head) + 1):
            for j in range(2):
                if PERM_AT[j] == i:
                    seq += perms[j]
            seq += head[i:i + 1]
        rest = turns[XHEAD:] + [task(lambda g=g: x_quant(1, g)) for g in range(2)]
        carry = []
        for phase in units:
            seq += weave([task(product_next) for a in phase], rest)
            g, ts, f0, w = phase[0]
            on_pe = len([1 for key in SUM_PE if key == (f0, g)])
            rest = carry + [
                task(lambda fb=fb, f0=f0, g=g: sum_on_pe(tiles[(f0, g)][1], tiles[(f0, g)][0], g, f0, fb))
                for fb in range(on_pe)
            ] + [
                task(
                    lambda fb=fb, f0=f0, g=g: add_base(tiles[(f0, g)][1], tiles[(f0, g)][0], g, f0, fb),
                    lambda fb=fb, f0=f0, g=g: base_bank(g, f0, fb),
                )
                for fb in range(on_pe, w // 128)
            ]
            carry = [task(lambda w=w, f0=f0, g=g: seal(f0, w, g))]
        seq += rest[1:] + rest[:1] + carry
        ahead = [(i, a) for i, (run, a) in enumerate(seq) if a]
        for i, (run, a) in enumerate(seq):
            while ahead and ahead[0][0] <= i + AHEAD:
                ahead.pop(0)[1]()
            run()
            for j in range(NMQ):
                if mq:
                    mq.pop(0)()
        while mq:
            mq.pop(0)()
